import numpy as np
import ml_dtypes


def mxq(x, axis, fmt="e4m3"):
    dtype, down = {"e4m3": (ml_dtypes.float8_e4m3fn, 7), "e5m2": (ml_dtypes.float8_e5m2, 14)}[fmt]
    v = np.moveaxis(np.asarray(x, np.float32).astype(ml_dtypes.bfloat16).astype(np.float64), axis, -1)
    blocks = v.reshape(v.shape[:-1] + (-1, 32))
    amax = np.abs(blocks).max(-1, keepdims=True)
    byte = np.maximum(np.where(amax > 0, np.frexp(amax)[1] - 1 + 127, 0) - down, 1)
    scale = np.exp2(byte - 127.0)
    codes = (blocks / scale).astype(np.float32).astype(dtype).astype(np.float64)
    return np.moveaxis((codes * scale).reshape(v.shape), -1, axis)


WIDE = False


def mx_kscale(k):
    if not WIDE:
        return np.ones(k)
    levels = np.array([10, -10, 5, -5, 0])
    if k % 512:
        return np.exp2(np.random.permutation(np.resize(levels, k // 32))).repeat(32)
    a = np.empty((k // 512, 16))
    for p in range(k // 512):
        a[p, :8] = np.random.permutation(np.resize(levels, 8))
        for g in range(8):
            far = levels[np.abs(levels - a[p, g]) >= 10]
            a[p, g + 8] = far[np.random.randint(len(far))]
    return np.exp2(a.ravel()).repeat(32)


def f64(x):
    return np.asarray(x).astype(np.float64)


E2M1 = np.array([0.0, 0.5, 1.0, 1.5, 2.0, 3.0, 4.0, 6.0, -0.0, -0.5, -1.0, -1.5, -2.0, -3.0, -4.0, -6.0])


def pack_weight(w, fmt):
    k, n = w.shape
    w = f64(np.asarray(w, np.float32).astype(ml_dtypes.bfloat16)).reshape(k // 32, 32, n)
    amax = np.abs(w).max(1)
    if fmt == "e4m3":
        byte = np.frexp(amax)[1] - 1 + 127 - 7
    else:
        mant, ex = np.frexp(amax / 6.0)
        byte = np.where(mant > 0.5, ex, ex - 1) + 127
    byte = np.clip(np.where(amax > 0, byte, 1), 1, 254)
    scaled = (w * np.exp2(127.0 - byte)[:, None, :]).reshape(k, n).astype(np.float32)
    by_word = np.ascontiguousarray(scaled.reshape(k // 512, 128, 4, n).transpose(0, 1, 3, 2))
    if fmt == "e4m3":
        words = by_word.astype(ml_dtypes.float8_e4m3fn).view(np.uint8)
    else:
        c = by_word.astype(ml_dtypes.float4_e2m1fn).view(np.uint8) & 0xF
        words = (c[..., 0::2] | (c[..., 1::2] << 4)).reshape(k // 512, 128, 2 * n)
    return np.ascontiguousarray(words), np.ascontiguousarray(byte.astype(np.uint8).reshape(k // 512, 16, n))


def unpack_weight(words, scales, fmt):
    g, _, n = scales.shape
    words = np.ascontiguousarray(words).reshape(g, 128, n, -1)
    if fmt == "e4m3":
        vals = words.view(ml_dtypes.float8_e4m3fn).astype(np.float64)
    else:
        nib = np.empty((g, 128, n, 4), np.uint8)
        nib[..., 0::2] = words & 0xF
        nib[..., 1::2] = words >> 4
        vals = E2M1[nib]
    vals = vals * np.repeat(np.exp2(scales.astype(np.float64) - 127.0), 8, axis=1)[..., None]
    return vals.transpose(0, 1, 3, 2).reshape(g * 512, n)


def planes(y):
    n, m = y.shape
    v = y.astype(np.float32).astype(ml_dtypes.bfloat16).astype(np.float64).reshape(n // 32, 32, m)
    top = np.abs(v).max(1)
    byte = np.clip(np.where(top > 0, np.frexp(top)[1] - 1 + 127 - 7, 1), 1, 254)
    codes = (v * np.exp2(127.0 - byte)[:, None, :]).reshape(n, m).astype(np.float32).astype(ml_dtypes.float8_e4m3fn).view(np.uint8)
    words = codes.reshape(n // 512, 128, 4, m).transpose(0, 1, 3, 2)
    return np.ascontiguousarray(words), np.ascontiguousarray(byte.astype(np.uint8).reshape(n // 512, 16, m))


def silu(v):
    return v / (1.0 + np.exp(-np.maximum(v, -700.0)))


O, K, R, M, T = 512, 1536, 512, 1536, 512


def setup_inputs():
    n = np.random.standard_normal
    s = mx_kscale(K)[:, None]
    u = mx_kscale(R)[:, None]
    x = n((K, T)); x[:O] *= 6.0
    w = n((K, M)) / np.sqrt(K) / s; w[:O] /= 2.0
    p_w8 = pack_weight(w[:O], "e4m3")
    p_w4 = pack_weight(w[O:], "e2m1")
    p_up = pack_weight(n((R, M)) / np.sqrt(R) / u, "e2m1")
    return {
        "x": (x * s).astype(np.float32),
        "w8_words": p_w8[0],
        "w8_scales": p_w8[1],
        "w4_words": p_w4[0],
        "w4_scales": p_w4[1],
        "down": (0.3 * n((K, R)) / np.sqrt(K) / s * u.T).astype(np.float32),
        "up_words": p_up[0],
        "up_scales": p_up[1],
        "b": (0.3 * n(1536)).astype(np.float32),
    }


def reference(x, w8_words, w8_scales, w4_words, w4_scales, down, up_words, up_scales, b):
    x_ = mxq(f64(x), 0, "e4m3")
    w8_ = unpack_weight(w8_words, w8_scales, "e4m3")
    w4_ = unpack_weight(w4_words, w4_scales, "e2m1")
    down_ = mxq(f64(down), 0, "e4m3")
    up_ = unpack_weight(up_words, up_scales, "e2m1")
    h_ = mxq(down_.T @ x_, 0, "e4m3")
    y = x_[:O].T @ w8_ + x_[O:].T @ w4_ + h_.T @ up_
    out_0 = silu(y + f64(b)[None, :])
    return (out_0,) + planes(out_0)

@@ -1,0 +1,312 @@
+from contextlib import ExitStack
+
+import concourse.mybir as mybir
+from concourse.masks import make_identity
+
+K, R, M, T = 1536, 512, 1536, 512
+FLOPS = 2 * (K * R * T + (K + R) * T * M)
+
+F32 = mybir.dt.float32
+BF16 = mybir.dt.bfloat16
+I32 = mybir.dt.int32
+U32 = mybir.dt.uint32
+U8 = mybir.dt.uint8
+FP8X4 = mybir.dt.float8_e4m3fn_x4
+FP4X4 = mybir.dt.float4_e2m1fn_x4
+ACT = mybir.ActivationFunctionType
+ADD = mybir.AluOpType.add
+
+P = 128
+PACK = 4
+K_PASS = P * PACK
+PASSES = K // K_PASS
+BANK = 512
+CHUNKS = M // BANK
+HALF = BANK // 2
+LAST_SCALAR_COLS = 84
+
+
+def tile_mix_three_tm_pl_silu_kernel(
+    tc, x, w8_words, w8_scales, w4_words, w4_scales, down, up_words, up_scales, b, out_0, out_1, out_2
+):
+    nc = tc.nc
+
+    with ExitStack() as ctx:
+        sb = ctx.enter_context(tc.tile_pool(name="sb", bufs=1))
+        ps = ctx.enter_context(tc.psum_pool(name="ps", bufs=1))
+        ctx.enter_context(tc.manual_schedule())
+
+        def sbuf(name, shape, dtype):
+            return sb.tile(shape, dtype, name=name, align_bytes=64)
+
+        banks = [ps.tile([P, BANK], F32, name="bank%d" % n) for n in range(8)]
+        first_banks, second_banks = banks[:4], banks[4:]
+
+        w8_plane = sbuf("w8_plane", [P, 1, M], U8)
+        w4_plane = sbuf("w4_plane", [P, 2, M], U8)
+        up_plane = sbuf("up_plane", [P, 1, M], U8)
+        for plane in (w8_plane, w4_plane, up_plane):
+            nc.vector.memset(plane[:].bitcast(U32), 0)
+
+        b_cols = sbuf("b_cols", [P, M // P], F32)
+        nc.scalar.dma_start(out=b_cols[:], in_=b.rearrange("(p c) -> p c", p=P))
+        identity = sbuf("identity", [P, P], F32)
+        make_identity(nc, identity[:])
+        for plane, scales in ((w8_plane, w8_scales), (w4_plane, w4_scales), (up_plane, up_scales)):
+            for q in range(4):
+                nc.gpsimd.dma_start(
+                    out=plane[32 * q : 32 * q + 4].bitcast(I32),
+                    in_=scales[:, 4 * q : 4 * q + 4, :].rearrange("a r n -> r a n").bitcast(I32),
+                )
+
+        def load_rows(name, src, a):
+            raw = sbuf("%s_raw%d" % (name, a), [P, PACK, T], F32)
+            rows = src[a * K_PASS : (a + 1) * K_PASS, :]
+            nc.sync.dma_start(out=raw[:], in_=rows.rearrange("(p j) w -> p j w", j=PACK))
+            return raw
+
+        def load_w8(c):
+            words = sbuf("w8_c%d" % c, [P, BANK], U32)
+            src = w8_words[0].rearrange("p n t -> p (n t)")[:, c * BANK * 4 : (c + 1) * BANK * 4]
+            nc.sync.dma_start(out=words[:].bitcast(I32), in_=src.bitcast(I32))
+            return words
+
+        def load_fp4(name, src, a0, a1, c0, c1):
+            words = sbuf(name, [P, a1 - a0, (c1 - c0) * BANK * 2], U8)
+            part = src[a0:a1, :, c0 * BANK * 2 : c1 * BANK * 2].rearrange("a p n -> p a n")
+            nc.sync.dma_start(out=words[:].bitcast(I32), in_=part.bitcast(I32))
+            return words
+
+        x_raw, down_raw = {}, {}
+        for a in range(PASSES - 1):
+            x_raw[a] = load_rows("x", x, a)
+            down_raw[a] = load_rows("down", down, a)
+        last = PASSES - 1
+        down_raw[last] = load_rows("down", down, last)
+        w8_sb = {0: load_w8(0)}
+        w4_sb = {(0, 0): load_fp4("w4_a0c0", w4_words, 0, 1, 0, 1)[:, 0, :]}
+        x_raw[last] = load_rows("x", x, last)
+        w4_sb[(1, 0)] = load_fp4("w4_a1c0", w4_words, 1, 2, 0, 1)[:, 0, :]
+        up_sb = load_fp4("up_all", up_words, 0, 1, 0, CHUNKS)[:, 0, :]
+        for c in range(1, CHUNKS):
+            w8_sb[c] = load_w8(c)
+            both = load_fp4("w4_c%d" % c, w4_words, 0, 2, c, c + 1)
+            w4_sb[(0, c)] = both[:, 0, :]
+            w4_sb[(1, c)] = both[:, 1, :]
+
+        bias = sbuf("bias", [P, M], F32)
+        for g in range(CHUNKS):
+            for c in range(4):
+                col = 4 * g + c
+                nc.tensor.transpose(
+                    first_banks[g][:, c * P : (c + 1) * P],
+                    b_cols[:, col : col + 1].to_broadcast([P, P]),
+                    identity[:],
+                )
+            nc.scalar.activation(
+                out=bias[:].rearrange("q (p g c) -> q g p c", g=CHUNKS, c=4)[:, g],
+                in_=first_banks[g][:].rearrange("q (c p) -> q p c", c=4),
+                func=ACT.Copy,
+            )
+
+        def quantise_pass(name, raw, scalar_cols):
+            codes = sbuf(name + "_codes", [P, T], U32)
+            plane = sbuf(name + "_plane", [P, T], U8)
+            src = raw[:].rearrange("p j (m h l) -> p h m j l", h=2, l=2)
+            halves = [sbuf("%s_bf%d" % (name, h), [P, 2 * K_PASS], BF16) for h in range(2)]
+            dst = [t[:].rearrange("p (l m j) -> p m j l", l=2, j=PACK) for t in halves]
+            nc.vector.tensor_copy(out=dst[0], in_=src[:, 0])
+            nc.scalar.copy(out=dst[1][:, :scalar_cols], in_=src[:, 1, :scalar_cols])
+            if scalar_cols < P:
+                nc.vector.tensor_copy(out=dst[1][:, scalar_cols:], in_=src[:, 1, scalar_cols:])
+            for h in range(2):
+                cols = slice(h * 2 * P, (h + 1) * 2 * P)
+                nc.vector.quantize_mx(out=codes[:, cols].bitcast(FP8X4), scales=plane[:, cols], in_=halves[h][:])
+            return codes, plane
+
+        x_q, down_q = {}, {}
+
+        def h_pass(a):
+            for i in range(4):
+                tok = slice(i * P, (i + 1) * P)
+                for j in range(4):
+                    rank = slice(j * P, (j + 1) * P)
+                    nc.tensor.matmul_mx(
+                        out=second_banks[i][:, rank],
+                        lhsT=down_q[a][0][:, rank].bitcast(FP8X4),
+                        lhsT_scale=down_q[a][1][:, rank],
+                        rhs=x_q[a][0][:, tok].bitcast(FP8X4),
+                        rhs_scale=x_q[a][1][:, tok],
+                        start=(a == 0 and j == 0),
+                        stop=(a == last and j == 3),
+                    )
+
+        h_codes = sbuf("h_codes", [P, T], U32)
+        h_plane = sbuf("h_plane", [P, T], U8)
+
+        def y_pass(s, i, n0, width, out):
+            c, off = divmod(n0, BANK)
+            tok = slice(i * P, (i + 1) * P)
+            cols = slice(n0, n0 + width)
+            if s == 0:
+                rhs, rhs_scale = w8_sb[c][:, off : off + width].bitcast(FP8X4), w8_plane[:, 0, cols]
+            elif s <= last:
+                rhs = w4_sb[(s - 1, c)][:, 2 * off : 2 * (off + width)].bitcast(FP4X4)
+                rhs_scale = w4_plane[:, s - 1, cols]
+            else:
+                rhs, rhs_scale = up_sb[:, 2 * n0 : 2 * (n0 + width)].bitcast(FP4X4), up_plane[:, 0, cols]
+            codes, plane = x_q[s] if s <= last else (h_codes, h_plane)
+            nc.tensor.matmul_mx(
+                out=out,
+                lhsT=codes[:, tok].bitcast(FP8X4),
+                lhsT_scale=plane[:, tok],
+                rhs=rhs,
+                rhs_scale=rhs_scale,
+                start=(s == 0),
+                stop=(s == PASSES),
+            )
+
+        for a in range(last):
+            x_q[a] = quantise_pass("x%d" % a, x_raw[a], P)
+            down_q[a] = quantise_pass("down%d" % a, down_raw[a], P)
+            h_pass(a)
+        down_q[last] = quantise_pass("down%d" % last, down_raw[last], P)
+        for s in range(last):
+            for i in range(4):
+                y_pass(s, i, 0, BANK, first_banks[i][:])
+        x_q[last] = quantise_pass("x%d" % last, x_raw[last], LAST_SCALAR_COLS)
+        h_pass(last)
+
+        h_bf = [sbuf("h_bf%d" % i, [P, K_PASS], BF16) for i in range(4)]
+
+        def h_copy(i, copy):
+            copy(
+                out=h_bf[i][:].rearrange("p (t j) -> p t j", j=PACK),
+                in_=second_banks[i][:].rearrange("p (j t) -> p t j", j=PACK),
+            )
+
+        def h_quantise(i):
+            tok = slice(i * P, (i + 1) * P)
+            nc.vector.quantize_mx(out=h_codes[:, tok].bitcast(FP8X4), scales=h_plane[:, tok], in_=h_bf[i][:])
+
+        h_copy(0, nc.scalar.copy)
+        h_copy(1, nc.vector.tensor_copy)
+        h_copy(2, nc.scalar.copy)
+        h_copy(3, nc.scalar.copy)
+        for i in range(4):
+            h_quantise(i)
+
+        blocks = [(0, BANK), (BANK, BANK), (2 * BANK, HALF), (2 * BANK + HALF, HALF)]
+        block_banks = [first_banks, second_banks, first_banks[:2], first_banks[2:]]
+        pre = [sbuf("pre%d" % n, [P, 4, w], F32) for n, (n0, w) in enumerate(blocks)]
+        res = [sbuf("res%d" % n, [P, 4, w], F32) for n, (n0, w) in enumerate(blocks)]
+        res_bf = [sbuf("res_bf%d" % u, [P, HALF * PACK], BF16) for u in range(M // HALF)]
+        out_codes = sbuf("out_codes", [P, M], U32)
+        out_plane = sbuf("out_plane", [P, M], U8)
+        out_rows = out_0.rearrange("(p i) n -> p i n", i=PACK)
+        out_words = out_1[0].rearrange("p n t -> p (n t)").bitcast(I32)
+
+        def multiply(n, k):
+            n0, w = blocks[n]
+            per = BANK // w
+            for e in range(per):
+                for s in range(PASSES + 1):
+                    y_pass(s, k * per + e, n0, w, block_banks[n][k][:, e * w : (e + 1) * w])
+
+        def add_bias(n, k):
+            n0, w = blocks[n]
+            per = BANK // w
+            nc.vector.tensor_tensor(
+                out=pre[n][:, k * per : (k + 1) * per, :],
+                in0=block_banks[n][k][:].rearrange("p (e w) -> p e w", e=per),
+                in1=bias[:, n0 : n0 + w].unsqueeze(1).to_broadcast([P, per, w]),
+                op=ADD,
+            )
+
+        def activate(n, k):
+            n0, w = blocks[n]
+            per = BANK // w
+            rows = slice(k * per, (k + 1) * per)
+            nc.scalar.activation(out=res[n][:, rows, :], in_=pre[n][:, rows, :], func=ACT.Silu)
+            nc.sync.dma_start(out=out_rows[:, rows, n0 : n0 + w], in_=res[n][:, rows, :])
+
+        def round_cols(n, lo, hi, copy):
+            n0 = blocks[n][0]
+            u, off = divmod(n0 + lo, HALF)
+            dst = res_bf[u][:, off * PACK : (off + hi - lo) * PACK]
+            copy(
+                out=dst.rearrange("p (c e i) -> p c i e", e=4, i=PACK),
+                in_=res[n][:, :, lo:hi].rearrange("p i (c e) -> p c i e", e=4),
+            )
+
+        def quantise_out(u):
+            cols = slice(u * HALF, (u + 1) * HALF)
+            nc.vector.quantize_mx(out=out_codes[:, cols].bitcast(FP8X4), scales=out_plane[:, cols], in_=res_bf[u][:])
+
+        def store_words(n0, n1):
+            nc.sync.dma_start(out=out_words[:, n0:n1], in_=out_codes[:, n0:n1].bitcast(I32))
+
+        def store_scales(n0, n1, queues):
+            for q in range(4):
+                queues[q].dma_start(
+                    out=out_2[0, 4 * q : 4 * q + 4, n0:n1].bitcast(I32),
+                    in_=out_plane[32 * q : 32 * q + 4, n0:n1].bitcast(I32),
+                )
+
+        on_vector, on_scalar = nc.vector.tensor_copy, nc.scalar.copy
+
+        y_pass(last, 0, 0, BANK, first_banks[0][:])
+        y_pass(last, 1, 0, BANK, first_banks[1][:])
+        y_pass(PASSES, 0, 0, BANK, first_banks[0][:])
+        y_pass(PASSES, 1, 0, BANK, first_banks[1][:])
+        for i in (2, 3):
+            y_pass(last, i, 0, BANK, first_banks[i][:])
+            y_pass(PASSES, i, 0, BANK, first_banks[i][:])
+        for k in range(4):
+            add_bias(0, k)
+            activate(0, k)
+
+        multiply(1, 0)
+        add_bias(1, 0)
+        activate(1, 0)
+        round_cols(0, 0, HALF, on_vector)
+        round_cols(0, HALF, BANK, on_scalar)
+        multiply(1, 1)
+        add_bias(1, 1)
+        activate(1, 1)
+        quantise_out(0)
+        multiply(1, 2)
+        add_bias(1, 2)
+        quantise_out(1)
+        store_words(0, BANK)
+        activate(1, 2)
+        multiply(1, 3)
+        add_bias(1, 3)
+        activate(1, 3)
+        round_cols(1, HALF, BANK, on_scalar)
+        multiply(2, 0)
+        add_bias(2, 0)
+        activate(2, 0)
+        round_cols(1, 0, HALF, on_vector)
+        multiply(2, 1)
+        add_bias(2, 1)
+        quantise_out(2)
+        quantise_out(3)
+        store_words(BANK, 2 * BANK)
+        store_scales(0, 2 * BANK, [nc.sync] * 4)
+        activate(2, 1)
+        round_cols(2, HALF // 2, HALF, on_scalar)
+        multiply(3, 0)
+        add_bias(3, 0)
+        activate(3, 0)
+        round_cols(2, 0, HALF // 2, on_vector)
+        multiply(3, 1)
+        add_bias(3, 1)
+        activate(3, 1)
+        quantise_out(4)
+        store_words(2 * BANK, 2 * BANK + HALF)
+        round_cols(3, 0, 168, on_vector)
+        round_cols(3, 168, HALF, on_scalar)
+        quantise_out(5)
+        store_words(2 * BANK + HALF, M)
+        store_scales(2 * BANK, M, [nc.scalar, nc.scalar, nc.sync, nc.sync])

@@ -24,6 +24,8 @@ BANK = 512
 CHUNKS = M // BANK
 HALF = BANK // 2
 LAST_SCALAR_COLS = 84
+H2 = HALF // 2
+FINAL_VECTOR_COLS = 168
 
 
 def tile_mix_three_tm_pl_silu_kernel(
@@ -42,21 +44,25 @@ def tile_mix_three_tm_pl_silu_kernel(
         banks = [ps.tile([P, BANK], F32, name="bank%d" % n) for n in range(8)]
         first_banks, second_banks = banks[:4], banks[4:]
 
-        w8_plane = sbuf("w8_plane", [P, 1, M], U8)
-        w4_plane = sbuf("w4_plane", [P, 2, M], U8)
-        up_plane = sbuf("up_plane", [P, 1, M], U8)
-        for plane in (w8_plane, w4_plane, up_plane):
+        def zeroed_plane(name, passes, width):
+            plane = sbuf(name, [P, passes, width], U8)
             nc.vector.memset(plane[:].bitcast(U32), 0)
+            return plane
+
+        w8_plane = zeroed_plane("w8_plane", 1, M)
+        w4_planes = [zeroed_plane("w4_plane0", 2, BANK), zeroed_plane("w4_plane1", 2, M - BANK)]
+        up_plane = zeroed_plane("up_plane", 1, M)
 
         b_cols = sbuf("b_cols", [P, M // P], F32)
         nc.scalar.dma_start(out=b_cols[:], in_=b.rearrange("(p c) -> p c", p=P))
         identity = sbuf("identity", [P, P], F32)
         make_identity(nc, identity[:])
-        for plane, scales in ((w8_plane, w8_scales), (w4_plane, w4_scales), (up_plane, up_scales)):
+
+        def load_scales(plane, scales, n0, n1):
             for q in range(4):
-                nc.gpsimd.dma_start(
+                nc.sync.dma_start(
                     out=plane[32 * q : 32 * q + 4].bitcast(I32),
-                    in_=scales[:, 4 * q : 4 * q + 4, :].rearrange("a r n -> r a n").bitcast(I32),
+                    in_=scales[:, 4 * q : 4 * q + 4, n0:n1].rearrange("a r n -> r a n").bitcast(I32),
                 )
 
         def load_rows(name, src, a):
@@ -77,22 +83,29 @@ def tile_mix_three_tm_pl_silu_kernel(
             nc.sync.dma_start(out=words[:].bitcast(I32), in_=part.bitcast(I32))
             return words
 
-        x_raw, down_raw = {}, {}
-        for a in range(PASSES - 1):
-            x_raw[a] = load_rows("x", x, a)
-            down_raw[a] = load_rows("down", down, a)
-        last = PASSES - 1
-        down_raw[last] = load_rows("down", down, last)
-        w8_sb = {0: load_w8(0)}
-        w4_sb = {(0, 0): load_fp4("w4_a0c0", w4_words, 0, 1, 0, 1)[:, 0, :]}
-        x_raw[last] = load_rows("x", x, last)
-        w4_sb[(1, 0)] = load_fp4("w4_a1c0", w4_words, 1, 2, 0, 1)[:, 0, :]
-        up_sb = load_fp4("up_all", up_words, 0, 1, 0, CHUNKS)[:, 0, :]
-        for c in range(1, CHUNKS):
-            w8_sb[c] = load_w8(c)
+        def load_w4(c):
             both = load_fp4("w4_c%d" % c, w4_words, 0, 2, c, c + 1)
-            w4_sb[(0, c)] = both[:, 0, :]
-            w4_sb[(1, c)] = both[:, 1, :]
+            return [both[:, 0, :], both[:, 1, :]]
+
+        last = PASSES - 1
+        x_raw, down_raw, w8_sb, w4_sb = {}, {}, {}, {}
+        x_raw[0] = load_rows("x", x, 0)
+        down_raw[0] = load_rows("down", down, 0)
+        load_scales(w8_plane, w8_scales, 0, M)
+        x_raw[1] = load_rows("x", x, 1)
+        load_scales(w4_planes[0], w4_scales, 0, BANK)
+        down_raw[1] = load_rows("down", down, 1)
+        down_raw[last] = load_rows("down", down, last)
+        w8_sb[0] = load_w8(0)
+        x_raw[last] = load_rows("x", x, last)
+        w4_sb[0] = [load_fp4("w4_a%dc0" % a, w4_words, a, a + 1, 0, 1)[:, 0, :] for a in range(2)]
+        load_scales(up_plane, up_scales, 0, M)
+        up_sb = load_fp4("up_all", up_words, 0, 1, 0, CHUNKS)[:, 0, :]
+        w8_sb[1] = load_w8(1)
+        load_scales(w4_planes[1], w4_scales, BANK, M)
+        w4_sb[1] = load_w4(1)
+        w8_sb[2] = load_w8(2)
+        w4_sb[2] = load_w4(2)
 
         bias = sbuf("bias", [P, M], F32)
         for g in range(CHUNKS):
@@ -103,10 +116,9 @@ def tile_mix_three_tm_pl_silu_kernel(
                     b_cols[:, col : col + 1].to_broadcast([P, P]),
                     identity[:],
                 )
-            nc.scalar.activation(
+            nc.scalar.copy(
                 out=bias[:].rearrange("q (p g c) -> q g p c", g=CHUNKS, c=4)[:, g],
                 in_=first_banks[g][:].rearrange("q (c p) -> q p c", c=4),
-                func=ACT.Copy,
             )
 
         def quantise_pass(name, raw, scalar_cols):
@@ -126,10 +138,10 @@ def tile_mix_three_tm_pl_silu_kernel(
 
         x_q, down_q = {}, {}
 
-        def h_pass(a):
+        def h_pass(a, ranks):
             for i in range(4):
                 tok = slice(i * P, (i + 1) * P)
-                for j in range(4):
+                for j in ranks:
                     rank = slice(j * P, (j + 1) * P)
                     nc.tensor.matmul_mx(
                         out=second_banks[i][:, rank],
@@ -144,38 +156,54 @@ def tile_mix_three_tm_pl_silu_kernel(
         h_codes = sbuf("h_codes", [P, T], U32)
         h_plane = sbuf("h_plane", [P, T], U8)
 
-        def y_pass(s, i, n0, width, out):
+        def y_bank(u, k):
+            return banks[(2 * u + k) % 8]
+
+        def y_out(u, i):
+            if u == M // HALF - 1 and i == 3:
+                return banks[4][:, :HALF]
+            return y_bank(u, i // 2)[:, (i % 2) * HALF : (i % 2 + 1) * HALF]
+
+        def y_pass(u, k, s, tiles=(0, 1)):
+            n0 = u * HALF
             c, off = divmod(n0, BANK)
-            tok = slice(i * P, (i + 1) * P)
-            cols = slice(n0, n0 + width)
+            cols = slice(n0, n0 + HALF)
+            part = min(c, 1)
+            part_cols = slice(n0 - part * BANK, n0 - part * BANK + HALF)
             if s == 0:
-                rhs, rhs_scale = w8_sb[c][:, off : off + width].bitcast(FP8X4), w8_plane[:, 0, cols]
+                rhs, rhs_scale = w8_sb[c][:, off : off + HALF].bitcast(FP8X4), w8_plane[:, 0, cols]
             elif s <= last:
-                rhs = w4_sb[(s - 1, c)][:, 2 * off : 2 * (off + width)].bitcast(FP4X4)
-                rhs_scale = w4_plane[:, s - 1, cols]
+                rhs = w4_sb[c][s - 1][:, 2 * off : 2 * (off + HALF)].bitcast(FP4X4)
+                rhs_scale = w4_planes[part][:, s - 1, part_cols]
             else:
-                rhs, rhs_scale = up_sb[:, 2 * n0 : 2 * (n0 + width)].bitcast(FP4X4), up_plane[:, 0, cols]
+                rhs, rhs_scale = up_sb[:, 2 * n0 : 2 * (n0 + HALF)].bitcast(FP4X4), up_plane[:, 0, cols]
             codes, plane = x_q[s] if s <= last else (h_codes, h_plane)
-            nc.tensor.matmul_mx(
-                out=out,
-                lhsT=codes[:, tok].bitcast(FP8X4),
-                lhsT_scale=plane[:, tok],
-                rhs=rhs,
-                rhs_scale=rhs_scale,
-                start=(s == 0),
-                stop=(s == PASSES),
-            )
+            for e in tiles:
+                tok = slice((2 * k + e) * P, (2 * k + e + 1) * P)
+                nc.tensor.matmul_mx(
+                    out=y_out(u, 2 * k + e),
+                    lhsT=codes[:, tok].bitcast(FP8X4),
+                    lhsT_scale=plane[:, tok],
+                    rhs=rhs,
+                    rhs_scale=rhs_scale,
+                    start=(s == 0 and e == tiles[0]),
+                    stop=(s == PASSES and e == tiles[-1]),
+                )
+
+        def early_pass(s):
+            for u in range(2):
+                for k in range(2):
+                    y_pass(u, k, s)
 
         for a in range(last):
             x_q[a] = quantise_pass("x%d" % a, x_raw[a], P)
             down_q[a] = quantise_pass("down%d" % a, down_raw[a], P)
-            h_pass(a)
+            h_pass(a, range(4))
         down_q[last] = quantise_pass("down%d" % last, down_raw[last], P)
-        for s in range(last):
-            for i in range(4):
-                y_pass(s, i, 0, BANK, first_banks[i][:])
+        early_pass(0)
+        early_pass(1)
         x_q[last] = quantise_pass("x%d" % last, x_raw[last], LAST_SCALAR_COLS)
-        h_pass(last)
+        h_pass(last, range(4))
 
         h_bf = [sbuf("h_bf%d" % i, [P, K_PASS], BF16) for i in range(4)]
 
@@ -192,56 +220,49 @@ def tile_mix_three_tm_pl_silu_kernel(
         h_copy(0, nc.scalar.copy)
         h_copy(1, nc.vector.tensor_copy)
         h_copy(2, nc.scalar.copy)
-        h_copy(3, nc.scalar.copy)
-        for i in range(4):
-            h_quantise(i)
+        h_quantise(0)
+        h_quantise(1)
+        h_copy(3, nc.vector.tensor_copy)
+        h_quantise(2)
+        h_quantise(3)
 
-        blocks = [(0, BANK), (BANK, BANK), (2 * BANK, HALF), (2 * BANK + HALF, HALF)]
-        block_banks = [first_banks, second_banks, first_banks[:2], first_banks[2:]]
-        pre = [sbuf("pre%d" % n, [P, 4, w], F32) for n, (n0, w) in enumerate(blocks)]
-        res = [sbuf("res%d" % n, [P, 4, w], F32) for n, (n0, w) in enumerate(blocks)]
-        res_bf = [sbuf("res_bf%d" % u, [P, HALF * PACK], BF16) for u in range(M // HALF)]
+        units = M // HALF
+        pre = [sbuf("pre%d" % u, [P, 4, HALF], F32) for u in range(units)]
+        res = [sbuf("res%d" % u, [P, 4, HALF], F32) for u in range(units)]
+        res_bf = sbuf("res_bf", [P, M * PACK], BF16)
         out_codes = sbuf("out_codes", [P, M], U32)
         out_plane = sbuf("out_plane", [P, M], U8)
         out_rows = out_0.rearrange("(p i) n -> p i n", i=PACK)
         out_words = out_1[0].rearrange("p n t -> p (n t)").bitcast(I32)
 
-        def multiply(n, k):
-            n0, w = blocks[n]
-            per = BANK // w
-            for e in range(per):
-                for s in range(PASSES + 1):
-                    y_pass(s, k * per + e, n0, w, block_banks[n][k][:, e * w : (e + 1) * w])
-
-        def add_bias(n, k):
-            n0, w = blocks[n]
-            per = BANK // w
+        def add_bias(u, i0, i1):
+            sums = y_out(u, i0) if i1 - i0 == 1 else y_bank(u, i0 // 2)[:]
             nc.vector.tensor_tensor(
-                out=pre[n][:, k * per : (k + 1) * per, :],
-                in0=block_banks[n][k][:].rearrange("p (e w) -> p e w", e=per),
-                in1=bias[:, n0 : n0 + w].unsqueeze(1).to_broadcast([P, per, w]),
+                out=pre[u][:, i0:i1, :],
+                in0=sums.rearrange("p (e w) -> p e w", w=HALF),
+                in1=bias[:, u * HALF : (u + 1) * HALF].unsqueeze(1).to_broadcast([P, i1 - i0, HALF]),
                 op=ADD,
             )
 
-        def activate(n, k):
-            n0, w = blocks[n]
-            per = BANK // w
-            rows = slice(k * per, (k + 1) * per)
-            nc.scalar.activation(out=res[n][:, rows, :], in_=pre[n][:, rows, :], func=ACT.Silu)
-            nc.sync.dma_start(out=out_rows[:, rows, n0 : n0 + w], in_=res[n][:, rows, :])
+        def activate(u, i0, i1):
+            nc.scalar.activation(out=res[u][:, i0:i1, :], in_=pre[u][:, i0:i1, :], func=ACT.Silu)
 
-        def round_cols(n, lo, hi, copy):
-            n0 = blocks[n][0]
-            u, off = divmod(n0 + lo, HALF)
-            dst = res_bf[u][:, off * PACK : (off + hi - lo) * PACK]
+        def store_rows(u, i0, i1):
+            nc.sync.dma_start(out=out_rows[:, i0:i1, u * HALF : (u + 1) * HALF], in_=res[u][:, i0:i1, :])
+
+        def round_cols(u, lo, hi, copy):
             copy(
-                out=dst.rearrange("p (c e i) -> p c i e", e=4, i=PACK),
-                in_=res[n][:, :, lo:hi].rearrange("p i (c e) -> p c i e", e=4),
+                out=res_bf[:, (u * HALF + lo) * PACK : (u * HALF + hi) * PACK].rearrange("p (c e i) -> p c i e", e=4, i=PACK),
+                in_=res[u][:, :, lo:hi].rearrange("p i (c e) -> p c i e", e=4),
             )
 
-        def quantise_out(u):
-            cols = slice(u * HALF, (u + 1) * HALF)
-            nc.vector.quantize_mx(out=out_codes[:, cols].bitcast(FP8X4), scales=out_plane[:, cols], in_=res_bf[u][:])
+        def quantise_out(u0, u1):
+            cols = slice(u0 * HALF, u1 * HALF)
+            nc.vector.quantize_mx(
+                out=out_codes[:, cols].bitcast(FP8X4),
+                scales=out_plane[:, cols],
+                in_=res_bf[:, u0 * HALF * PACK : u1 * HALF * PACK],
+            )
 
         def store_words(n0, n1):
             nc.sync.dma_start(out=out_words[:, n0:n1], in_=out_codes[:, n0:n1].bitcast(I32))
@@ -255,58 +276,60 @@ def tile_mix_three_tm_pl_silu_kernel(
 
         on_vector, on_scalar = nc.vector.tensor_copy, nc.scalar.copy
 
-        y_pass(last, 0, 0, BANK, first_banks[0][:])
-        y_pass(last, 1, 0, BANK, first_banks[1][:])
-        y_pass(PASSES, 0, 0, BANK, first_banks[0][:])
-        y_pass(PASSES, 1, 0, BANK, first_banks[1][:])
-        for i in (2, 3):
-            y_pass(last, i, 0, BANK, first_banks[i][:])
-            y_pass(PASSES, i, 0, BANK, first_banks[i][:])
-        for k in range(4):
-            add_bias(0, k)
-            activate(0, k)
+        def finish(u, k, first):
+            for s in range(first, PASSES + 1):
+                y_pass(u, k, s)
 
-        multiply(1, 0)
-        add_bias(1, 0)
-        activate(1, 0)
+        def epilogue(u, k):
+            add_bias(u, 2 * k, 2 * k + 2)
+            activate(u, 2 * k, 2 * k + 2)
+            store_rows(u, 2 * k, 2 * k + 2)
+
+        early_pass(last)
+        for k in range(2):
+            for u in range(2):
+                y_pass(u, k, PASSES)
+        for k in range(2):
+            for u in range(2):
+                epilogue(u, k)
+        finish(2, 0, 0)
+        epilogue(2, 0)
         round_cols(0, 0, HALF, on_vector)
-        round_cols(0, HALF, BANK, on_scalar)
-        multiply(1, 1)
-        add_bias(1, 1)
-        activate(1, 1)
-        quantise_out(0)
-        multiply(1, 2)
-        add_bias(1, 2)
-        quantise_out(1)
-        store_words(0, BANK)
-        activate(1, 2)
-        multiply(1, 3)
-        add_bias(1, 3)
-        activate(1, 3)
-        round_cols(1, HALF, BANK, on_scalar)
-        multiply(2, 0)
-        add_bias(2, 0)
-        activate(2, 0)
-        round_cols(1, 0, HALF, on_vector)
-        multiply(2, 1)
-        add_bias(2, 1)
-        quantise_out(2)
-        quantise_out(3)
-        store_words(BANK, 2 * BANK)
-        store_scales(0, 2 * BANK, [nc.sync] * 4)
-        activate(2, 1)
-        round_cols(2, HALF // 2, HALF, on_scalar)
-        multiply(3, 0)
-        add_bias(3, 0)
-        activate(3, 0)
-        round_cols(2, 0, HALF // 2, on_vector)
-        multiply(3, 1)
-        add_bias(3, 1)
-        activate(3, 1)
-        quantise_out(4)
-        store_words(2 * BANK, 2 * BANK + HALF)
-        round_cols(3, 0, 168, on_vector)
-        round_cols(3, 168, HALF, on_scalar)
-        quantise_out(5)
-        store_words(2 * BANK + HALF, M)
-        store_scales(2 * BANK, M, [nc.scalar, nc.scalar, nc.sync, nc.sync])
+        finish(2, 1, 0)
+        epilogue(2, 1)
+        round_cols(1, H2, HALF, on_scalar)
+        round_cols(1, 0, H2, on_vector)
+        finish(3, 0, 0)
+        epilogue(3, 0)
+        round_cols(2, 0, H2, on_scalar)
+        finish(3, 1, 0)
+        epilogue(3, 1)
+        round_cols(2, H2, HALF, on_scalar)
+        quantise_out(0, 2)
+        store_words(0, 2 * HALF)
+        finish(4, 0, 0)
+        epilogue(4, 0)
+        round_cols(3, 0, HALF, on_vector)
+        finish(4, 1, 0)
+        epilogue(4, 1)
+        round_cols(4, H2, HALF, on_scalar)
+        quantise_out(2, 4)
+        store_words(2 * HALF, 4 * HALF)
+        store_scales(0, 4 * HALF, [nc.sync] * 4)
+        final = units - 1
+        finish(final, 0, 0)
+        epilogue(final, 0)
+        round_cols(final - 1, 0, H2, on_vector)
+        for i in (2, 3):
+            for s in range(PASSES + 1):
+                y_pass(final, 1, s, (i % 2,))
+            add_bias(final, i, i + 1)
+            activate(final, i, i + 1)
+        quantise_out(final - 1, final)
+        store_words((final - 1) * HALF, final * HALF)
+        store_rows(final, 2, 4)
+        round_cols(final, 0, FINAL_VECTOR_COLS, on_vector)
+        round_cols(final, FINAL_VECTOR_COLS, HALF, on_scalar)
+        quantise_out(final, units)
+        store_words(final * HALF, M)
+        store_scales((final - 1) * HALF, M, [nc.scalar, nc.scalar, nc.sync, nc.sync])

@@ -23,9 +23,9 @@ PASSES = K // K_PASS
 BANK = 512
 CHUNKS = M // BANK
 HALF = BANK // 2
+SCALAR_COLS = 96
 LAST_SCALAR_COLS = 84
-H2 = HALF // 2
-FINAL_VECTOR_COLS = 168
+FINAL_VECTOR_COLS = 112
 
 
 def tile_mix_three_tm_pl_silu_kernel(
@@ -49,7 +49,7 @@ def tile_mix_three_tm_pl_silu_kernel(
             nc.vector.memset(plane[:].bitcast(U32), 0)
             return plane
 
-        w8_plane = zeroed_plane("w8_plane", 1, M)
+        w8_planes = [zeroed_plane("w8_plane0", 1, BANK), zeroed_plane("w8_plane1", 1, M - BANK)]
         w4_planes = [zeroed_plane("w4_plane0", 2, BANK), zeroed_plane("w4_plane1", 2, M - BANK)]
         up_plane = zeroed_plane("up_plane", 1, M)
 
@@ -59,7 +59,7 @@ def tile_mix_three_tm_pl_silu_kernel(
         make_identity(nc, identity[:])
 
         def load_scales(plane, scales, n0, n1):
-            for q in range(4):
+            for q in (0, 2, 1, 3):
                 nc.sync.dma_start(
                     out=plane[32 * q : 32 * q + 4].bitcast(I32),
                     in_=scales[:, 4 * q : 4 * q + 4, n0:n1].rearrange("a r n -> r a n").bitcast(I32),
@@ -91,7 +91,7 @@ def tile_mix_three_tm_pl_silu_kernel(
         x_raw, down_raw, w8_sb, w4_sb = {}, {}, {}, {}
         x_raw[0] = load_rows("x", x, 0)
         down_raw[0] = load_rows("down", down, 0)
-        load_scales(w8_plane, w8_scales, 0, M)
+        load_scales(w8_planes[0], w8_scales, 0, BANK)
         x_raw[1] = load_rows("x", x, 1)
         load_scales(w4_planes[0], w4_scales, 0, BANK)
         down_raw[1] = load_rows("down", down, 1)
@@ -100,10 +100,12 @@ def tile_mix_three_tm_pl_silu_kernel(
         x_raw[last] = load_rows("x", x, last)
         w4_sb[0] = [load_fp4("w4_a%dc0" % a, w4_words, a, a + 1, 0, 1)[:, 0, :] for a in range(2)]
         load_scales(up_plane, up_scales, 0, M)
-        up_sb = load_fp4("up_all", up_words, 0, 1, 0, CHUNKS)[:, 0, :]
+        up_sb = [load_fp4("up_first", up_words, 0, 1, 0, 1)[:, 0, :]]
+        load_scales(w8_planes[1], w8_scales, BANK, M)
         w8_sb[1] = load_w8(1)
         load_scales(w4_planes[1], w4_scales, BANK, M)
         w4_sb[1] = load_w4(1)
+        up_sb.append(load_fp4("up_rest", up_words, 0, 1, 1, CHUNKS)[:, 0, :])
         w8_sb[2] = load_w8(2)
         w4_sb[2] = load_w4(2)
 
@@ -156,50 +158,55 @@ def tile_mix_three_tm_pl_silu_kernel(
         h_codes = sbuf("h_codes", [P, T], U32)
         h_plane = sbuf("h_plane", [P, T], U8)
 
-        def y_bank(u, k):
-            return banks[(2 * u + k) % 8]
+        blocks = [(0, BANK), (BANK, BANK), (2 * BANK, HALF), (2 * BANK + HALF, HALF)]
+        groups = []
+        for i in range(4):
+            groups.append((0, (i,), first_banks[i]))
+        for i in range(4):
+            groups.append((1, (i,), second_banks[i]))
+        groups.append((2, (0, 1), first_banks[0]))
+        groups.append((2, (2, 3), first_banks[1]))
+        groups.append((3, (0, 1), first_banks[2]))
+        groups.append((3, (2,), first_banks[3]))
+        groups.append((3, (3,), second_banks[0]))
 
-        def y_out(u, i):
-            if u == M // HALF - 1 and i == 3:
-                return banks[4][:, :HALF]
-            return y_bank(u, i // 2)[:, (i % 2) * HALF : (i % 2 + 1) * HALF]
-
-        def y_pass(u, k, s, tiles=(0, 1)):
-            n0 = u * HALF
+        def y_pass(g, s):
+            n, tiles, bank = groups[g]
+            n0, width = blocks[n]
             c, off = divmod(n0, BANK)
-            cols = slice(n0, n0 + HALF)
+            cols = slice(n0, n0 + width)
             part = min(c, 1)
-            part_cols = slice(n0 - part * BANK, n0 - part * BANK + HALF)
+            part_cols = slice(n0 - part * BANK, n0 - part * BANK + width)
             if s == 0:
-                rhs, rhs_scale = w8_sb[c][:, off : off + HALF].bitcast(FP8X4), w8_plane[:, 0, cols]
+                rhs, rhs_scale = w8_sb[c][:, off : off + width].bitcast(FP8X4), w8_planes[part][:, 0, part_cols]
             elif s <= last:
-                rhs = w4_sb[c][s - 1][:, 2 * off : 2 * (off + HALF)].bitcast(FP4X4)
+                rhs = w4_sb[c][s - 1][:, 2 * off : 2 * (off + width)].bitcast(FP4X4)
                 rhs_scale = w4_planes[part][:, s - 1, part_cols]
             else:
-                rhs, rhs_scale = up_sb[:, 2 * n0 : 2 * (n0 + HALF)].bitcast(FP4X4), up_plane[:, 0, cols]
+                rhs = up_sb[part][:, 2 * part_cols.start : 2 * part_cols.stop].bitcast(FP4X4)
+                rhs_scale = up_plane[:, 0, cols]
             codes, plane = x_q[s] if s <= last else (h_codes, h_plane)
-            for e in tiles:
-                tok = slice((2 * k + e) * P, (2 * k + e + 1) * P)
+            for e, i in enumerate(tiles):
+                tok = slice(i * P, (i + 1) * P)
                 nc.tensor.matmul_mx(
-                    out=y_out(u, 2 * k + e),
+                    out=bank[:, e * width : (e + 1) * width],
                     lhsT=codes[:, tok].bitcast(FP8X4),
                     lhsT_scale=plane[:, tok],
                     rhs=rhs,
                     rhs_scale=rhs_scale,
-                    start=(s == 0 and e == tiles[0]),
-                    stop=(s == PASSES and e == tiles[-1]),
+                    start=(s == 0 and e == 0),
+                    stop=(s == PASSES and e == len(tiles) - 1),
                 )
 
         def early_pass(s):
-            for u in range(2):
-                for k in range(2):
-                    y_pass(u, k, s)
+            for g in range(4):
+                y_pass(g, s)
 
         for a in range(last):
-            x_q[a] = quantise_pass("x%d" % a, x_raw[a], P)
-            down_q[a] = quantise_pass("down%d" % a, down_raw[a], P)
+            x_q[a] = quantise_pass("x%d" % a, x_raw[a], SCALAR_COLS)
+            down_q[a] = quantise_pass("down%d" % a, down_raw[a], SCALAR_COLS)
             h_pass(a, range(4))
-        down_q[last] = quantise_pass("down%d" % last, down_raw[last], P)
+        down_q[last] = quantise_pass("down%d" % last, down_raw[last], SCALAR_COLS)
         early_pass(0)
         early_pass(1)
         x_q[last] = quantise_pass("x%d" % last, x_raw[last], LAST_SCALAR_COLS)
@@ -226,49 +233,54 @@ def tile_mix_three_tm_pl_silu_kernel(
         h_quantise(2)
         h_quantise(3)
 
-        units = M // HALF
-        pre = [sbuf("pre%d" % u, [P, 4, HALF], F32) for u in range(units)]
-        res = [sbuf("res%d" % u, [P, 4, HALF], F32) for u in range(units)]
+        pre = [sbuf("pre%d" % n, [P, 4, w], F32) for n, (n0, w) in enumerate(blocks)]
+        res = [sbuf("res%d" % n, [P, 4, w], F32) for n, (n0, w) in enumerate(blocks)]
         res_bf = sbuf("res_bf", [P, M * PACK], BF16)
         out_codes = sbuf("out_codes", [P, M], U32)
         out_plane = sbuf("out_plane", [P, M], U8)
         out_rows = out_0.rearrange("(p i) n -> p i n", i=PACK)
         out_words = out_1[0].rearrange("p n t -> p (n t)").bitcast(I32)
 
-        def add_bias(u, i0, i1):
-            sums = y_out(u, i0) if i1 - i0 == 1 else y_bank(u, i0 // 2)[:]
+        def store_rows(n, i0, i1):
+            n0, w = blocks[n]
+            nc.sync.dma_start(out=out_rows[:, i0:i1, n0 : n0 + w], in_=res[n][:, i0:i1, :])
+
+        def epilogue(g, first_pass=0, store=True):
+            for s in range(first_pass, PASSES + 1):
+                y_pass(g, s)
+            n, tiles, bank = groups[g]
+            n0, w = blocks[n]
+            i0, i1 = tiles[0], tiles[-1] + 1
             nc.vector.tensor_tensor(
-                out=pre[u][:, i0:i1, :],
-                in0=sums.rearrange("p (e w) -> p e w", w=HALF),
-                in1=bias[:, u * HALF : (u + 1) * HALF].unsqueeze(1).to_broadcast([P, i1 - i0, HALF]),
+                out=pre[n][:, i0:i1, :],
+                in0=bank[:, : len(tiles) * w].rearrange("p (e w) -> p e w", w=w),
+                in1=bias[:, n0 : n0 + w].unsqueeze(1).to_broadcast([P, len(tiles), w]),
                 op=ADD,
             )
+            nc.scalar.activation(out=res[n][:, i0:i1, :], in_=pre[n][:, i0:i1, :], func=ACT.Silu)
+            if store:
+                store_rows(n, i0, i1)
 
-        def activate(u, i0, i1):
-            nc.scalar.activation(out=res[u][:, i0:i1, :], in_=pre[u][:, i0:i1, :], func=ACT.Silu)
-
-        def store_rows(u, i0, i1):
-            nc.sync.dma_start(out=out_rows[:, i0:i1, u * HALF : (u + 1) * HALF], in_=res[u][:, i0:i1, :])
-
-        def round_cols(u, lo, hi, copy):
+        def round_cols(lo, hi, copy):
+            n = max(m for m, (n0, w) in enumerate(blocks) if n0 <= lo)
+            n0 = blocks[n][0]
             copy(
-                out=res_bf[:, (u * HALF + lo) * PACK : (u * HALF + hi) * PACK].rearrange("p (c e i) -> p c i e", e=4, i=PACK),
-                in_=res[u][:, :, lo:hi].rearrange("p i (c e) -> p c i e", e=4),
+                out=res_bf[:, lo * PACK : hi * PACK].rearrange("p (c e i) -> p c i e", e=4, i=PACK),
+                in_=res[n][:, :, lo - n0 : hi - n0].rearrange("p i (c e) -> p c i e", e=4),
             )
 
-        def quantise_out(u0, u1):
-            cols = slice(u0 * HALF, u1 * HALF)
+        def quantise_out(n0, n1):
             nc.vector.quantize_mx(
-                out=out_codes[:, cols].bitcast(FP8X4),
-                scales=out_plane[:, cols],
-                in_=res_bf[:, u0 * HALF * PACK : u1 * HALF * PACK],
+                out=out_codes[:, n0:n1].bitcast(FP8X4),
+                scales=out_plane[:, n0:n1],
+                in_=res_bf[:, n0 * PACK : n1 * PACK],
             )
 
         def store_words(n0, n1):
             nc.sync.dma_start(out=out_words[:, n0:n1], in_=out_codes[:, n0:n1].bitcast(I32))
 
         def store_scales(n0, n1, queues):
-            for q in range(4):
+            for q in (0, 2, 1, 3):
                 queues[q].dma_start(
                     out=out_2[0, 4 * q : 4 * q + 4, n0:n1].bitcast(I32),
                     in_=out_plane[32 * q : 32 * q + 4, n0:n1].bitcast(I32),
@@ -276,60 +288,37 @@ def tile_mix_three_tm_pl_silu_kernel(
 
         on_vector, on_scalar = nc.vector.tensor_copy, nc.scalar.copy
 
-        def finish(u, k, first):
-            for s in range(first, PASSES + 1):
-                y_pass(u, k, s)
-
-        def epilogue(u, k):
-            add_bias(u, 2 * k, 2 * k + 2)
-            activate(u, 2 * k, 2 * k + 2)
-            store_rows(u, 2 * k, 2 * k + 2)
-
         early_pass(last)
-        for k in range(2):
-            for u in range(2):
-                y_pass(u, k, PASSES)
-        for k in range(2):
-            for u in range(2):
-                epilogue(u, k)
-        finish(2, 0, 0)
-        epilogue(2, 0)
-        round_cols(0, 0, HALF, on_vector)
-        finish(2, 1, 0)
-        epilogue(2, 1)
-        round_cols(1, H2, HALF, on_scalar)
-        round_cols(1, 0, H2, on_vector)
-        finish(3, 0, 0)
-        epilogue(3, 0)
-        round_cols(2, 0, H2, on_scalar)
-        finish(3, 1, 0)
-        epilogue(3, 1)
-        round_cols(2, H2, HALF, on_scalar)
-        quantise_out(0, 2)
-        store_words(0, 2 * HALF)
-        finish(4, 0, 0)
-        epilogue(4, 0)
-        round_cols(3, 0, HALF, on_vector)
-        finish(4, 1, 0)
-        epilogue(4, 1)
-        round_cols(4, H2, HALF, on_scalar)
-        quantise_out(2, 4)
-        store_words(2 * HALF, 4 * HALF)
-        store_scales(0, 4 * HALF, [nc.sync] * 4)
-        final = units - 1
-        finish(final, 0, 0)
-        epilogue(final, 0)
-        round_cols(final - 1, 0, H2, on_vector)
-        for i in (2, 3):
-            for s in range(PASSES + 1):
-                y_pass(final, 1, s, (i % 2,))
-            add_bias(final, i, i + 1)
-            activate(final, i, i + 1)
-        quantise_out(final - 1, final)
-        store_words((final - 1) * HALF, final * HALF)
-        store_rows(final, 2, 4)
-        round_cols(final, 0, FINAL_VECTOR_COLS, on_vector)
-        round_cols(final, FINAL_VECTOR_COLS, HALF, on_scalar)
-        quantise_out(final, units)
-        store_words(final * HALF, M)
-        store_scales((final - 1) * HALF, M, [nc.scalar, nc.scalar, nc.sync, nc.sync])
+        for g in range(4):
+            epilogue(g, PASSES)
+        epilogue(4)
+        epilogue(5)
+        round_cols(0, 256, on_vector)
+        round_cols(384, 512, on_scalar)
+        epilogue(6)
+        round_cols(256, 384, on_vector)
+        epilogue(7)
+        quantise_out(0, 512)
+        store_words(0, 512)
+        round_cols(512, 640, on_scalar)
+        epilogue(8)
+        round_cols(640, 768, on_scalar)
+        round_cols(768, 1024, on_vector)
+        epilogue(9)
+        quantise_out(768, 1024)
+        epilogue(10, 0, False)
+        quantise_out(512, 768)
+        store_words(512, 1024)
+        store_scales(0, 1024, [nc.sync] * 4)
+        store_rows(3, 0, 2)
+        epilogue(11, 0, False)
+        epilogue(12, 0, False)
+        round_cols(1024, 1280, on_vector)
+        store_rows(3, 2, 4)
+        quantise_out(1024, 1280)
+        store_words(1024, 1280)
+        round_cols(1280, 1280 + FINAL_VECTOR_COLS, on_vector)
+        round_cols(1280 + FINAL_VECTOR_COLS, M, on_scalar)
+        quantise_out(1280, M)
+        store_words(1280, M)
+        store_scales(1024, M, [nc.scalar, nc.sync, nc.scalar, nc.sync])

@@ -23,6 +23,7 @@ PASSES = K // K_PASS
 BANK = 512
 CHUNKS = M // BANK
 HALF = BANK // 2
+W8_ROW = 4
 SCALAR_COLS = 96
 LAST_SCALAR_COLS = 84
 FINAL_VECTOR_COLS = 112
@@ -49,7 +50,7 @@ def tile_mix_three_tm_pl_silu_kernel(
             nc.vector.memset(plane[:].bitcast(U32), 0)
             return plane
 
-        w8_planes = [zeroed_plane("w8_plane0", 1, BANK), zeroed_plane("w8_plane1", 1, M - BANK)]
+        w8_plane = zeroed_plane("w8_plane", 1, M)
         w4_planes = [zeroed_plane("w4_plane0", 2, BANK), zeroed_plane("w4_plane1", 2, M - BANK)]
         up_plane = zeroed_plane("up_plane", 1, M)
 
@@ -58,10 +59,10 @@ def tile_mix_three_tm_pl_silu_kernel(
         identity = sbuf("identity", [P, P], F32)
         make_identity(nc, identity[:])
 
-        def load_scales(plane, scales, n0, n1):
+        def load_scales(plane, scales, n0, n1, queue=nc.sync, row=0):
             for q in (0, 2, 1, 3):
-                nc.sync.dma_start(
-                    out=plane[32 * q : 32 * q + 4].bitcast(I32),
+                queue.dma_start(
+                    out=plane[32 * q + row : 32 * q + row + 4].bitcast(I32),
                     in_=scales[:, 4 * q : 4 * q + 4, n0:n1].rearrange("a r n -> r a n").bitcast(I32),
                 )
 
@@ -87,11 +88,11 @@ def tile_mix_three_tm_pl_silu_kernel(
             both = load_fp4("w4_c%d" % c, w4_words, 0, 2, c, c + 1)
             return [both[:, 0, :], both[:, 1, :]]
 
+        load_scales(w8_plane, w8_scales, 0, M, nc.gpsimd, W8_ROW)
         last = PASSES - 1
         x_raw, down_raw, w8_sb, w4_sb = {}, {}, {}, {}
         x_raw[0] = load_rows("x", x, 0)
         down_raw[0] = load_rows("down", down, 0)
-        load_scales(w8_planes[0], w8_scales, 0, BANK)
         x_raw[1] = load_rows("x", x, 1)
         load_scales(w4_planes[0], w4_scales, 0, BANK)
         down_raw[1] = load_rows("down", down, 1)
@@ -101,7 +102,6 @@ def tile_mix_three_tm_pl_silu_kernel(
         w4_sb[0] = [load_fp4("w4_a%dc0" % a, w4_words, a, a + 1, 0, 1)[:, 0, :] for a in range(2)]
         load_scales(up_plane, up_scales, 0, M)
         up_sb = [load_fp4("up_first", up_words, 0, 1, 0, 1)[:, 0, :]]
-        load_scales(w8_planes[1], w8_scales, BANK, M)
         w8_sb[1] = load_w8(1)
         load_scales(w4_planes[1], w4_scales, BANK, M)
         w4_sb[1] = load_w4(1)
@@ -178,7 +178,7 @@ def tile_mix_three_tm_pl_silu_kernel(
             part = min(c, 1)
             part_cols = slice(n0 - part * BANK, n0 - part * BANK + width)
             if s == 0:
-                rhs, rhs_scale = w8_sb[c][:, off : off + width].bitcast(FP8X4), w8_planes[part][:, 0, part_cols]
+                rhs, rhs_scale = w8_sb[c][:, off : off + width].bitcast(FP8X4), w8_plane[W8_ROW:, 0, cols]
             elif s <= last:
                 rhs = w4_sb[c][s - 1][:, 2 * off : 2 * (off + width)].bitcast(FP4X4)
                 rhs_scale = w4_planes[part][:, s - 1, part_cols]
@@ -300,6 +300,7 @@ def tile_mix_three_tm_pl_silu_kernel(
         epilogue(7)
         quantise_out(0, 512)
         store_words(0, 512)
+        store_scales(0, 512, [nc.sync] * 4)
         round_cols(512, 640, on_scalar)
         epilogue(8)
         round_cols(640, 768, on_scalar)
@@ -309,16 +310,14 @@ def tile_mix_three_tm_pl_silu_kernel(
         epilogue(10, 0, False)
         quantise_out(512, 768)
         store_words(512, 1024)
-        store_scales(0, 1024, [nc.sync] * 4)
         store_rows(3, 0, 2)
         epilogue(11, 0, False)
         epilogue(12, 0, False)
         round_cols(1024, 1280, on_vector)
         store_rows(3, 2, 4)
         quantise_out(1024, 1280)
-        store_words(1024, 1280)
         round_cols(1280, 1280 + FINAL_VECTOR_COLS, on_vector)
         round_cols(1280 + FINAL_VECTOR_COLS, M, on_scalar)
         quantise_out(1280, M)
-        store_words(1280, M)
-        store_scales(1024, M, [nc.scalar, nc.sync, nc.scalar, nc.sync])
+        store_words(1024, M)
+        store_scales(512, M, [nc.scalar, nc.sync, nc.scalar, nc.sync])

from contextlib import ExitStack

import concourse.mybir as mybir
from concourse.masks import make_identity

K, R, M, T = 1536, 512, 1536, 512
FLOPS = 2 * (K * R * T + (K + R) * T * M)

F32 = mybir.dt.float32
BF16 = mybir.dt.bfloat16
I32 = mybir.dt.int32
U32 = mybir.dt.uint32
U8 = mybir.dt.uint8
FP8X4 = mybir.dt.float8_e4m3fn_x4
FP4X4 = mybir.dt.float4_e2m1fn_x4
ACT = mybir.ActivationFunctionType
ADD = mybir.AluOpType.add

P = 128
PACK = 4
K_PASS = P * PACK
PASSES = K // K_PASS
BANK = 512
CHUNKS = M // BANK
HALF = BANK // 2
W8_ROW = 4
SCALAR_COLS = 96
LAST_SCALAR_COLS = 84
FINAL_VECTOR_COLS = 112


def tile_mix_three_tm_pl_silu_kernel(
    tc, x, w8_words, w8_scales, w4_words, w4_scales, down, up_words, up_scales, b, out_0, out_1, out_2
):
    nc = tc.nc

    with ExitStack() as ctx:
        sb = ctx.enter_context(tc.tile_pool(name="sb", bufs=1))
        ps = ctx.enter_context(tc.psum_pool(name="ps", bufs=1))
        ctx.enter_context(tc.manual_schedule())

        def sbuf(name, shape, dtype):
            return sb.tile(shape, dtype, name=name, align_bytes=64)

        banks = [ps.tile([P, BANK], F32, name="bank%d" % n) for n in range(8)]
        first_banks, second_banks = banks[:4], banks[4:]

        def zeroed_plane(name, passes, width):
            plane = sbuf(name, [P, passes, width], U8)
            nc.vector.memset(plane[:].bitcast(U32), 0)
            return plane

        w8_plane = zeroed_plane("w8_plane", 1, M)
        w4_planes = [zeroed_plane("w4_plane0", 2, BANK), zeroed_plane("w4_plane1", 2, M - BANK)]
        up_plane = zeroed_plane("up_plane", 1, M)

        b_cols = sbuf("b_cols", [P, M // P], F32)
        nc.scalar.dma_start(out=b_cols[:], in_=b.rearrange("(p c) -> p c", p=P))
        identity = sbuf("identity", [P, P], F32)
        make_identity(nc, identity[:])

        def load_scales(plane, scales, n0, n1, queue=nc.sync, row=0):
            for q in (0, 2, 1, 3):
                queue.dma_start(
                    out=plane[32 * q + row : 32 * q + row + 4].bitcast(I32),
                    in_=scales[:, 4 * q : 4 * q + 4, n0:n1].rearrange("a r n -> r a n").bitcast(I32),
                )

        def load_rows(name, src, a):
            raw = sbuf("%s_raw%d" % (name, a), [P, PACK, T], F32)
            rows = src[a * K_PASS : (a + 1) * K_PASS, :]
            nc.sync.dma_start(out=raw[:], in_=rows.rearrange("(p j) w -> p j w", j=PACK))
            return raw

        def load_w8(c):
            words = sbuf("w8_c%d" % c, [P, BANK], U32)
            src = w8_words[0].rearrange("p n t -> p (n t)")[:, c * BANK * 4 : (c + 1) * BANK * 4]
            nc.sync.dma_start(out=words[:].bitcast(I32), in_=src.bitcast(I32))
            return words

        def load_fp4(name, src, a0, a1, c0, c1):
            words = sbuf(name, [P, a1 - a0, (c1 - c0) * BANK * 2], U8)
            part = src[a0:a1, :, c0 * BANK * 2 : c1 * BANK * 2].rearrange("a p n -> p a n")
            nc.sync.dma_start(out=words[:].bitcast(I32), in_=part.bitcast(I32))
            return words

        def load_w4(c):
            both = load_fp4("w4_c%d" % c, w4_words, 0, 2, c, c + 1)
            return [both[:, 0, :], both[:, 1, :]]

        load_scales(w8_plane, w8_scales, 0, M, nc.gpsimd, W8_ROW)
        last = PASSES - 1
        x_raw, down_raw, w8_sb, w4_sb = {}, {}, {}, {}
        x_raw[0] = load_rows("x", x, 0)
        down_raw[0] = load_rows("down", down, 0)
        x_raw[1] = load_rows("x", x, 1)
        load_scales(w4_planes[0], w4_scales, 0, BANK)
        down_raw[1] = load_rows("down", down, 1)
        down_raw[last] = load_rows("down", down, last)
        w8_sb[0] = load_w8(0)
        x_raw[last] = load_rows("x", x, last)
        w4_sb[0] = [load_fp4("w4_a%dc0" % a, w4_words, a, a + 1, 0, 1)[:, 0, :] for a in range(2)]
        load_scales(up_plane, up_scales, 0, M)
        up_sb = [load_fp4("up_first", up_words, 0, 1, 0, 1)[:, 0, :]]
        w8_sb[1] = load_w8(1)
        load_scales(w4_planes[1], w4_scales, BANK, M)
        w4_sb[1] = load_w4(1)
        up_sb.append(load_fp4("up_rest", up_words, 0, 1, 1, CHUNKS)[:, 0, :])
        w8_sb[2] = load_w8(2)
        w4_sb[2] = load_w4(2)

        bias = sbuf("bias", [P, M], F32)
        for g in range(CHUNKS):
            for c in range(4):
                col = 4 * g + c
                nc.tensor.transpose(
                    first_banks[g][:, c * P : (c + 1) * P],
                    b_cols[:, col : col + 1].to_broadcast([P, P]),
                    identity[:],
                )
            nc.scalar.copy(
                out=bias[:].rearrange("q (p g c) -> q g p c", g=CHUNKS, c=4)[:, g],
                in_=first_banks[g][:].rearrange("q (c p) -> q p c", c=4),
            )

        def quantise_pass(name, raw, scalar_cols):
            codes = sbuf(name + "_codes", [P, T], U32)
            plane = sbuf(name + "_plane", [P, T], U8)
            src = raw[:].rearrange("p j (m h l) -> p h m j l", h=2, l=2)
            halves = [sbuf("%s_bf%d" % (name, h), [P, 2 * K_PASS], BF16) for h in range(2)]
            dst = [t[:].rearrange("p (l m j) -> p m j l", l=2, j=PACK) for t in halves]
            nc.vector.tensor_copy(out=dst[0], in_=src[:, 0])
            nc.scalar.copy(out=dst[1][:, :scalar_cols], in_=src[:, 1, :scalar_cols])
            if scalar_cols < P:
                nc.vector.tensor_copy(out=dst[1][:, scalar_cols:], in_=src[:, 1, scalar_cols:])
            for h in range(2):
                cols = slice(h * 2 * P, (h + 1) * 2 * P)
                nc.vector.quantize_mx(out=codes[:, cols].bitcast(FP8X4), scales=plane[:, cols], in_=halves[h][:])
            return codes, plane

        x_q, down_q = {}, {}

        def h_pass(a, ranks):
            for i in range(4):
                tok = slice(i * P, (i + 1) * P)
                for j in ranks:
                    rank = slice(j * P, (j + 1) * P)
                    nc.tensor.matmul_mx(
                        out=second_banks[i][:, rank],
                        lhsT=down_q[a][0][:, rank].bitcast(FP8X4),
                        lhsT_scale=down_q[a][1][:, rank],
                        rhs=x_q[a][0][:, tok].bitcast(FP8X4),
                        rhs_scale=x_q[a][1][:, tok],
                        start=(a == 0 and j == 0),
                        stop=(a == last and j == 3),
                    )

        h_codes = sbuf("h_codes", [P, T], U32)
        h_plane = sbuf("h_plane", [P, T], U8)

        blocks = [(0, BANK), (BANK, BANK), (2 * BANK, HALF), (2 * BANK + HALF, HALF)]
        groups = []
        for i in range(4):
            groups.append((0, (i,), first_banks[i]))
        for i in range(4):
            groups.append((1, (i,), second_banks[i]))
        groups.append((2, (0, 1), first_banks[0]))
        groups.append((2, (2, 3), first_banks[1]))
        groups.append((3, (0, 1), first_banks[2]))
        groups.append((3, (2,), first_banks[3]))
        groups.append((3, (3,), second_banks[0]))

        def y_pass(g, s):
            n, tiles, bank = groups[g]
            n0, width = blocks[n]
            c, off = divmod(n0, BANK)
            cols = slice(n0, n0 + width)
            part = min(c, 1)
            part_cols = slice(n0 - part * BANK, n0 - part * BANK + width)
            if s == 0:
                rhs, rhs_scale = w8_sb[c][:, off : off + width].bitcast(FP8X4), w8_plane[W8_ROW:, 0, cols]
            elif s <= last:
                rhs = w4_sb[c][s - 1][:, 2 * off : 2 * (off + width)].bitcast(FP4X4)
                rhs_scale = w4_planes[part][:, s - 1, part_cols]
            else:
                rhs = up_sb[part][:, 2 * part_cols.start : 2 * part_cols.stop].bitcast(FP4X4)
                rhs_scale = up_plane[:, 0, cols]
            codes, plane = x_q[s] if s <= last else (h_codes, h_plane)
            for e, i in enumerate(tiles):
                tok = slice(i * P, (i + 1) * P)
                nc.tensor.matmul_mx(
                    out=bank[:, e * width : (e + 1) * width],
                    lhsT=codes[:, tok].bitcast(FP8X4),
                    lhsT_scale=plane[:, tok],
                    rhs=rhs,
                    rhs_scale=rhs_scale,
                    start=(s == 0 and e == 0),
                    stop=(s == PASSES and e == len(tiles) - 1),
                )

        def early_pass(s):
            for g in range(4):
                y_pass(g, s)

        for a in range(last):
            x_q[a] = quantise_pass("x%d" % a, x_raw[a], SCALAR_COLS)
            down_q[a] = quantise_pass("down%d" % a, down_raw[a], SCALAR_COLS)
            h_pass(a, range(4))
        down_q[last] = quantise_pass("down%d" % last, down_raw[last], SCALAR_COLS)
        early_pass(0)
        early_pass(1)
        x_q[last] = quantise_pass("x%d" % last, x_raw[last], LAST_SCALAR_COLS)
        h_pass(last, range(4))

        h_bf = [sbuf("h_bf%d" % i, [P, K_PASS], BF16) for i in range(4)]

        def h_copy(i, copy):
            copy(
                out=h_bf[i][:].rearrange("p (t j) -> p t j", j=PACK),
                in_=second_banks[i][:].rearrange("p (j t) -> p t j", j=PACK),
            )

        def h_quantise(i):
            tok = slice(i * P, (i + 1) * P)
            nc.vector.quantize_mx(out=h_codes[:, tok].bitcast(FP8X4), scales=h_plane[:, tok], in_=h_bf[i][:])

        h_copy(0, nc.scalar.copy)
        h_copy(1, nc.vector.tensor_copy)
        h_copy(2, nc.scalar.copy)
        h_quantise(0)
        h_quantise(1)
        h_copy(3, nc.vector.tensor_copy)
        h_quantise(2)
        h_quantise(3)

        pre = [sbuf("pre%d" % n, [P, 4, w], F32) for n, (n0, w) in enumerate(blocks)]
        res = [sbuf("res%d" % n, [P, 4, w], F32) for n, (n0, w) in enumerate(blocks)]
        res_bf = sbuf("res_bf", [P, M * PACK], BF16)
        out_codes = sbuf("out_codes", [P, M], U32)
        out_plane = sbuf("out_plane", [P, M], U8)
        out_rows = out_0.rearrange("(p i) n -> p i n", i=PACK)
        out_words = out_1[0].rearrange("p n t -> p (n t)").bitcast(I32)

        def store_rows(n, i0, i1):
            n0, w = blocks[n]
            nc.sync.dma_start(out=out_rows[:, i0:i1, n0 : n0 + w], in_=res[n][:, i0:i1, :])

        def epilogue(g, first_pass=0, store=True):
            for s in range(first_pass, PASSES + 1):
                y_pass(g, s)
            n, tiles, bank = groups[g]
            n0, w = blocks[n]
            i0, i1 = tiles[0], tiles[-1] + 1
            nc.vector.tensor_tensor(
                out=pre[n][:, i0:i1, :],
                in0=bank[:, : len(tiles) * w].rearrange("p (e w) -> p e w", w=w),
                in1=bias[:, n0 : n0 + w].unsqueeze(1).to_broadcast([P, len(tiles), w]),
                op=ADD,
            )
            nc.scalar.activation(out=res[n][:, i0:i1, :], in_=pre[n][:, i0:i1, :], func=ACT.Silu)
            if store:
                store_rows(n, i0, i1)

        def round_cols(lo, hi, copy):
            n = max(m for m, (n0, w) in enumerate(blocks) if n0 <= lo)
            n0 = blocks[n][0]
            copy(
                out=res_bf[:, lo * PACK : hi * PACK].rearrange("p (c e i) -> p c i e", e=4, i=PACK),
                in_=res[n][:, :, lo - n0 : hi - n0].rearrange("p i (c e) -> p c i e", e=4),
            )

        def quantise_out(n0, n1):
            nc.vector.quantize_mx(
                out=out_codes[:, n0:n1].bitcast(FP8X4),
                scales=out_plane[:, n0:n1],
                in_=res_bf[:, n0 * PACK : n1 * PACK],
            )

        def store_words(n0, n1):
            nc.sync.dma_start(out=out_words[:, n0:n1], in_=out_codes[:, n0:n1].bitcast(I32))

        def store_scales(n0, n1, queues):
            for q in (0, 2, 1, 3):
                queues[q].dma_start(
                    out=out_2[0, 4 * q : 4 * q + 4, n0:n1].bitcast(I32),
                    in_=out_plane[32 * q : 32 * q + 4, n0:n1].bitcast(I32),
                )

        on_vector, on_scalar = nc.vector.tensor_copy, nc.scalar.copy

        early_pass(last)
        for g in range(4):
            epilogue(g, PASSES)
        epilogue(4)
        epilogue(5)
        round_cols(0, 256, on_vector)
        round_cols(384, 512, on_scalar)
        epilogue(6)
        round_cols(256, 384, on_vector)
        epilogue(7)
        quantise_out(0, 512)
        store_words(0, 512)
        store_scales(0, 512, [nc.sync] * 4)
        round_cols(512, 640, on_scalar)
        epilogue(8)
        round_cols(640, 768, on_scalar)
        round_cols(768, 1024, on_vector)
        epilogue(9)
        quantise_out(768, 1024)
        epilogue(10, 0, False)
        quantise_out(512, 768)
        store_words(512, 1024)
        store_rows(3, 0, 2)
        epilogue(11, 0, False)
        epilogue(12, 0, False)
        round_cols(1024, 1280, on_vector)
        store_rows(3, 2, 4)
        quantise_out(1024, 1280)
        round_cols(1280, 1280 + FINAL_VECTOR_COLS, on_vector)
        round_cols(1280 + FINAL_VECTOR_COLS, M, on_scalar)
        quantise_out(1280, M)
        store_words(1024, M)
        store_scales(512, M, [nc.scalar, nc.sync, nc.scalar, nc.sync])
